import numpy as np
import ml_dtypes


def mxq(x, axis, fmt="e4m3"):
    dtype, down = {"e4m3": (ml_dtypes.float8_e4m3fn, 7), "e5m2": (ml_dtypes.float8_e5m2, 14)}[fmt]
    v = np.moveaxis(np.asarray(x, np.float32).astype(ml_dtypes.bfloat16).astype(np.float64), axis, -1)
    blocks = v.reshape(v.shape[:-1] + (-1, 32))
    amax = np.abs(blocks).max(-1, keepdims=True)
    byte = np.maximum(np.where(amax > 0, np.frexp(amax)[1] - 1 + 127, 0) - down, 1)
    scale = np.exp2(byte - 127.0)
    codes = (blocks / scale).astype(np.float32).astype(dtype).astype(np.float64)
    return np.moveaxis((codes * scale).reshape(v.shape), -1, axis)


WIDE = False


def mx_kscale(k):
    if not WIDE:
        return np.ones(k)
    levels = np.array([10, -10, 5, -5, 0])
    if k % 512:
        return np.exp2(np.random.permutation(np.resize(levels, k // 32))).repeat(32)
    a = np.empty((k // 512, 16))
    for p in range(k // 512):
        a[p, :8] = np.random.permutation(np.resize(levels, 8))
        for g in range(8):
            far = levels[np.abs(levels - a[p, g]) >= 10]
            a[p, g + 8] = far[np.random.randint(len(far))]
    return np.exp2(a.ravel()).repeat(32)


def f64(x):
    return np.asarray(x).astype(np.float64)


def striped(idx):
    return np.tile(np.asarray(idx).reshape(-1, 16).T, (8, 1)).astype(np.uint16)


def unstriped(offs):
    return offs[:16].T.reshape(-1).astype(np.int64)


E2M1 = np.array([0.0, 0.5, 1.0, 1.5, 2.0, 3.0, 4.0, 6.0, -0.0, -0.5, -1.0, -1.5, -2.0, -3.0, -4.0, -6.0])


def pack_weight(w, fmt):
    k, n = w.shape
    w = f64(np.asarray(w, np.float32).astype(ml_dtypes.bfloat16)).reshape(k // 32, 32, n)
    amax = np.abs(w).max(1)
    if fmt == "e4m3":
        byte = np.frexp(amax)[1] - 1 + 127 - 7
    else:
        mant, ex = np.frexp(amax / 6.0)
        byte = np.where(mant > 0.5, ex, ex - 1) + 127
    byte = np.clip(np.where(amax > 0, byte, 1), 1, 254)
    scaled = (w * np.exp2(127.0 - byte)[:, None, :]).reshape(k, n).astype(np.float32)
    by_word = np.ascontiguousarray(scaled.reshape(k // 512, 128, 4, n).transpose(0, 1, 3, 2))
    if fmt == "e4m3":
        words = by_word.astype(ml_dtypes.float8_e4m3fn).view(np.uint8)
    else:
        c = by_word.astype(ml_dtypes.float4_e2m1fn).view(np.uint8) & 0xF
        words = (c[..., 0::2] | (c[..., 1::2] << 4)).reshape(k // 512, 128, 2 * n)
    return np.ascontiguousarray(words), np.ascontiguousarray(byte.astype(np.uint8).reshape(k // 512, 16, n))


def unpack_weight(words, scales, fmt):
    g, _, n = scales.shape
    words = np.ascontiguousarray(words).reshape(g, 128, n, -1)
    if fmt == "e4m3":
        vals = words.view(ml_dtypes.float8_e4m3fn).astype(np.float64)
    else:
        nib = np.empty((g, 128, n, 4), np.uint8)
        nib[..., 0::2] = words & 0xF
        nib[..., 1::2] = words >> 4
        vals = E2M1[nib]
    vals = vals * np.repeat(np.exp2(scales.astype(np.float64) - 127.0), 8, axis=1)[..., None]
    return vals.transpose(0, 1, 3, 2).reshape(g * 512, n)


D, T, I, Q, E, N = 512, 2048, 512, 128, 512, 64


def setup_inputs():
    n = np.random.standard_normal
    idx = np.random.permutation(T)[:I]
    fd = mx_kscale(D)
    fi = mx_kscale(I)
    ti = np.ones(T)
    ti[idx] = fi
    keysp = pack_weight(n((D, T)) / fd[:, None], "e4m3")
    return {
        "query": (n((D, Q)) * 0.585 / np.sqrt(D) * fd[:, None]).astype(np.float32),
        "keys_words": keysp[0],
        "keys_scales": keysp[1],
        "lam": (np.random.uniform(0.4, 0.9, (Q, 1))).astype(np.float32),
        "sharp": (np.random.uniform(1.5, 3.0, (Q, 1))).astype(np.float32),
        "share": (np.random.uniform(0.5, 0.9, (Q, 1))).astype(np.float32),
        "os": (np.random.uniform(4.0, 16.0, (1, I)) * fi).astype(np.float32),
        "vals": (n((E, T)) / ti).astype(np.float32),
        "target": (n((Q, E))).astype(np.float32),
        "offs": striped(idx),
    }


def reference(query, keys_words, keys_scales, lam, sharp, share, os, vals, target, offs):
    idx = unstriped(offs)
    keysu = unpack_weight(keys_words, keys_scales, "e4m3")
    queryq = mxq(f64(query), 0, "e4m3")
    keysidxg = keysu[:, idx]
    a = queryq.T @ keysidxg
    mb = a.reshape(Q, N, I // N).max(axis=2)
    mr = np.repeat(mb, I // N, axis=1)
    s = a - mr * f64(lam)
    p = np.exp(s - np.max(s, axis=1, keepdims=True))
    r = p / np.sum(p, axis=1, keepdims=True)
    s2 = s * f64(sharp)
    p2 = np.exp(s2 - np.max(s2, axis=1, keepdims=True))
    r2 = p2 / np.sum(p2, axis=1, keepdims=True)
    w = r * f64(share) - r2 * (1.0 - f64(share))
    wo1 = w * f64(os)
    wt1 = wo1.T
    vt1 = f64(vals)[:, idx].T
    wt1q = mxq(wt1, 0, "e4m3")
    vt1q = mxq(vt1, 0, "e4m3")
    o = wt1q.T @ vt1q
    rs = f64(target) - o
    k2 = np.sqrt(np.mean(np.square(rs), axis=1, keepdims=True) + 0.5)
    y = rs / k2
    return y

from contextlib import ExitStack

import concourse.mybir as mybir
from concourse.masks import make_identity

D, T, I, Q, E, PAGES = 512, 2048, 512, 128, 512, 64
FLOPS = 2 * D * Q * I + 2 * I * Q * E

F32 = mybir.dt.float32
BF16 = mybir.dt.bfloat16
I32 = mybir.dt.int32
U32 = mybir.dt.uint32
U16 = mybir.dt.uint16
U8 = mybir.dt.uint8
FP8X4 = mybir.dt.float8_e4m3fn_x4
ALU = mybir.AluOpType
ACT = mybir.ActivationFunctionType
AXIS = mybir.AxisListType

P = 128
PACK = 4
CHUNKS = E // P
LIST_COLS = I // 16
VECTOR_COLS = 16
SPLIT = 320


def tile_attend_pagegap_twoheats_remainder_kernel(
    tc, query, keys_words, keys_scales, lam, sharp, share, slot_factor, vals, target, offs, out
):
    nc = tc.nc
    with ExitStack() as ctx:
        sb = ctx.enter_context(tc.tile_pool(name="sb", bufs=1))
        psum = ctx.enter_context(tc.psum_pool(name="psum", bufs=1))

        offsets = sb.tile([P, LIST_COLS], U16, name="offsets")
        q_raw = sb.tile([P, PACK, Q], F32, name="q_raw")
        key_scale_pool = sb.tile([P, T], U8, name="key_scale_pool")
        key_word_pool = sb.tile([P, T], U32, name="key_word_pool")
        val_pools = [sb.tile([P, T], F32, name=f"val_pool{c}", tag=f"val_pool{c}", align_bytes=64) for c in range(CHUNKS)]
        target_sb = sb.tile([P, E], F32, name="target_sb")
        lam_sb = sb.tile([P, 1], F32, name="lam_sb")
        sharp_sb = sb.tile([P, 1], F32, name="sharp_sb")
        share_sb = sb.tile([P, 1], F32, name="share_sb")
        factor_sb = sb.tile([P, PACK], F32, name="factor_sb")

        nc.vector.memset(key_scale_pool[:].bitcast(I32), 0)
        nc.sync.dma_start(offsets[:], offs)
        nc.sync.dma_start(q_raw[:], query.rearrange("(p j) q -> p j q", j=PACK))
        for quad in range(4):
            nc.sync.dma_start(
                key_scale_pool[32 * quad : 32 * quad + 4, :].bitcast(I32),
                keys_scales[0, 4 * quad : 4 * quad + 4, :].bitcast(I32),
            )
        nc.sync.dma_start(key_word_pool[:].bitcast(I32), keys_words[0].rearrange("p n t -> p (n t)").bitcast(I32))
        nc.sync.dma_start(val_pools[0][:], vals[:P, :])
        nc.sync.dma_start(lam_sb[:], lam)
        nc.sync.dma_start(sharp_sb[:], sharp)
        nc.sync.dma_start(share_sb[:], share)
        nc.sync.dma_start(factor_sb[:], slot_factor.rearrange("o (p t) -> p (o t)", t=PACK))
        for c in range(1, CHUNKS):
            nc.sync.dma_start(val_pools[c][:], vals[c * P : (c + 1) * P, :])
        nc.sync.dma_start(target_sb[:], target)

        ident = sb.tile([P, P], F32, name="ident")
        make_identity(nc, ident[:])
        lam_less_1 = sb.tile([P, 1], F32, name="lam_less_1")
        share_less_1 = sb.tile([P, 1], F32, name="share_less_1")
        nc.vector.tensor_scalar(lam_less_1[:], lam_sb[:], 1.0, -1.0, ALU.mult, ALU.add)
        nc.vector.tensor_scalar(share_less_1[:], share_sb[:], 1.0, -1.0, ALU.mult, ALU.add)

        q_grouped = sb.tile([P, Q, PACK], BF16, name="q_grouped", align_bytes=64)
        q_codes = sb.tile([P, Q], U32, name="q_codes", align_bytes=64)
        q_scales = sb.tile([P, Q], U8, name="q_scales", align_bytes=64)
        nc.scalar.activation(q_grouped[:], q_raw[:].rearrange("p j q -> p q j"), ACT.Copy)
        nc.vector.quantize_mx(q_codes[:].bitcast(FP8X4), q_scales[:], q_grouped[:].rearrange("p q j -> p (q j)"))

        key_scales = sb.tile([P, I], U8, name="key_scales", align_bytes=64)
        key_words = sb.tile([P, I], U32, name="key_words", align_bytes=64)
        nc.vector.tensor_copy(key_scales[:], key_scale_pool[:].indirect(offsets[:]))
        nc.vector.tensor_copy(key_words[:], key_word_pool[:].indirect(offsets[:]))
        scores = psum.tile([P, I], F32, name="scores", tag="turned0")
        nc.tensor.matmul_mx(
            scores[:], lhsT=q_codes[:].bitcast(FP8X4), lhsT_scale=q_scales[:],
            rhs=key_words[:].bitcast(FP8X4), rhs_scale=key_scales[:], start=True, stop=True,
        )

        page_max = sb.tile([P, PAGES], F32, name="page_max")
        page_gap = sb.tile([P, PAGES], F32, name="page_gap")
        page_low = sb.tile([P, PAGES], F32, name="page_low")
        bias1 = sb.tile([P, 1], F32, name="bias1")
        bias2 = sb.tile([P, 1], F32, name="bias2")
        neg_s = sb.tile([P, I], F32, name="neg_s")
        neg_s2 = sb.tile([P, I], F32, name="neg_s2", tag="picked1", align_bytes=64)
        nc.vector.tensor_reduce(page_max[:], scores[:].rearrange("p (n g) -> p n g", n=PAGES), AXIS.X, ALU.max)
        nc.vector.tensor_scalar(page_gap[:], page_max[:], lam_sb[:], None, ALU.mult)
        nc.vector.tensor_scalar(page_low[:], page_max[:], lam_less_1[:], None, ALU.mult, ALU.min, accum_out=bias1[:])
        nc.vector.tensor_tensor(
            neg_s[:].rearrange("p (t n j) -> p t n j", t=PACK, j=2),
            page_gap[:].rearrange("p (a n b) -> p a n b", a=1, b=1).to_broadcast([P, PACK, PAGES, 2]),
            scores[:].rearrange("p (n j t) -> p t n j", t=PACK, j=2),
            ALU.subtract,
        )
        p1 = sb.tile([P, I], F32, name="p1", tag="v_grouped0", align_bytes=64)
        p2 = sb.tile([P, I], F32, name="p2", tag="picked2", align_bytes=64)
        sum1 = sb.tile([P, 1], F32, name="sum1")
        sum2 = sb.tile([P, 1], F32, name="sum2")
        nc.scalar.activation(p1[:], neg_s[:], ACT.Exp, bias=bias1[:], scale=-1.0, accum_out=sum1[:])
        nc.vector.tensor_scalar(neg_s2[:], neg_s[:], sharp_sb[:], None, ALU.mult, ALU.min, accum_out=bias2[:])
        nc.scalar.activation(p2[:], neg_s2[:], ACT.Exp, bias=bias2[:], scale=-1.0, accum_out=sum2[:])
        inv1 = sb.tile([P, 1], F32, name="inv1")
        inv2 = sb.tile([P, 1], F32, name="inv2")
        w_plus = sb.tile([P, I], F32, name="w_plus")
        w_minus = sb.tile([P, I], F32, name="w_minus")
        nc.vector.reciprocal(inv1[:], sum1[:])
        nc.vector.tensor_scalar(w_plus[:], p1[:], inv1[:], share_sb[:], ALU.mult, ALU.mult)
        nc.vector.reciprocal(inv2[:], sum2[:])
        nc.vector.tensor_scalar(w_minus[:], p2[:], inv2[:], share_less_1[:], ALU.mult, ALU.mult)
        w_turned = psum.tile([P, PACK, Q], F32, name="w_turned")
        for part, term in enumerate((w_plus, w_minus)):
            for t in range(PACK):
                nc.tensor.matmul(
                    w_turned[:, t, :], term[:, t * P : (t + 1) * P], ident[:], is_transpose=True,
                    start=(part == 0 and t == 0), stop=(part == 1 and t == PACK - 1),
                )
        w_codes = sb.tile([P, Q], U32, name="w_codes", align_bytes=64)
        w_scales = sb.tile([P, Q], U8, name="w_scales", align_bytes=64)

        def weights_quantise():
            w_grouped = sb.tile([P, Q, PACK], BF16, name="w_grouped", tag="val_pool2", align_bytes=64)
            nc.vector.tensor_tensor(
                w_grouped[:],
                w_turned[:].rearrange("p t q -> p q t"),
                factor_sb[:].rearrange("p (a t) -> p a t", a=1).to_broadcast([P, Q, PACK]),
                ALU.mult,
            )
            nc.vector.quantize_mx(w_codes[:].bitcast(FP8X4), w_scales[:], w_grouped[:].rearrange("p q t -> p (q t)"))

        def gather_and_turn(c, turned, tag, cut):
            picked = sb.tile([P, I], BF16, name=f"picked{c}", tag=tag, align_bytes=64)
            if cut:
                nc.vector.tensor_copy(picked[:, : 16 * cut], val_pools[c][:].indirect(offsets[:, :cut]))
            nc.scalar.activation(picked[:, 16 * cut :], val_pools[c][:].indirect(offsets[:, cut:]), ACT.Copy)
            words = picked[:].bitcast(F32)
            for u in range(2):
                nc.tensor.transpose(turned[:, u, :], words[:, u : I // 2 : 2], ident[:])
            return picked

        def quantise(first, count, turned, copy):
            width = count * P
            grouped = sb.tile([P, width, PACK], BF16, name=f"v_grouped{first}", tag=f"v_grouped{first}", align_bytes=64)
            codes = sb.tile([P, width], U32, name=f"v_codes{first}", align_bytes=64)
            scales = sb.tile([P, width], U8, name=f"v_scales{first}", align_bytes=64)
            copy(
                grouped[:].bitcast(F32).rearrange("p (c e) u -> p c e u", c=count),
                turned[:].rearrange("p c u e -> p c e u"),
            )
            nc.vector.quantize_mx(codes[:].bitcast(FP8X4), scales[:], grouped[:].rearrange("p e t -> p (e t)"))
            return codes, scales

        def product(acc, codes, scales):
            nc.tensor.matmul_mx(
                acc, lhsT=w_codes[:].bitcast(FP8X4), lhsT_scale=w_scales[:],
                rhs=codes[:].bitcast(FP8X4), rhs_scale=scales[:], start=True, stop=True,
            )

        early = (CHUNKS - 1) * P
        turned0 = psum.tile([P, 1, 2, P], F32, name="turned0", tag="turned0")
        gather_and_turn(0, turned0[:, 0], "picked0", 0)
        v0 = quantise(0, 1, turned0, nc.vector.tensor_copy)
        turned12 = psum.tile([P, 2, 2, P], F32, name="turned12", tag="turned12")
        gather_and_turn(1, turned12[:, 0], "picked1", 0)
        gather_and_turn(2, turned12[:, 1], "picked2", VECTOR_COLS)
        weights_quantise()
        v12 = quantise(1, 2, turned12, nc.scalar.copy)
        o_early = psum.tile([P, early], F32, name="o_early", tag="turned12")
        product(o_early[:, :P], *v0)
        product(o_early[:, P:], *v12)
        turned3 = psum.tile([P, 1, 2, P], F32, name="turned3")
        picked = gather_and_turn(3, turned3[:, 0], "picked3", VECTOR_COLS)
        v3 = quantise(3, 1, turned3, nc.scalar.copy)
        o_last = psum.tile([P, P], F32, name="o_last")
        product(o_last[:], *v3)

        rest = sb.tile([P, E], F32, name="rest")
        squares = sb.tile([P, E], F32, name="squares")
        ssq_early = sb.tile([P, 1], F32, name="ssq_early")
        ssq_last = sb.tile([P, 1], F32, name="ssq_last")
        base = sb.tile([P, 1], F32, name="base")
        inv_norm = sb.tile([P, 1], F32, name="inv_norm")
        result = sb.tile([P, E], F32, name="result")
        nc.vector.tensor_tensor(rest[:, :early], target_sb[:, :early], o_early[:], ALU.subtract)
        nc.vector.scalar_tensor_tensor(
            squares[:, :early], rest[:, :early], 1.0, rest[:, :early], ALU.mult, ALU.mult, accum_out=ssq_early[:]
        )
        nc.vector.tensor_scalar(base[:], ssq_early[:], 1.0 / E, 0.5, ALU.mult, ALU.add)
        nc.vector.tensor_tensor(rest[:, early:], target_sb[:, early:], o_last[:], ALU.subtract)
        nc.vector.scalar_tensor_tensor(
            squares[:, early:], rest[:, early:], 1.0, rest[:, early:], ALU.mult, ALU.mult, accum_out=ssq_last[:]
        )
        nc.scalar.activation(inv_norm[:], ssq_last[:], ACT.Abs_reciprocal_sqrt, bias=base[:], scale=1.0 / E)
        nc.scalar.activation(result[:, SPLIT:], rest[:, SPLIT:], ACT.Copy, scale=inv_norm[:])
        nc.scalar.dma_start(out[:, SPLIT:], result[:, SPLIT:])
        nc.vector.tensor_scalar(result[:, :SPLIT], rest[:, :SPLIT], inv_norm[:], None, ALU.mult)
        nc.sync.dma_start(out[:, :SPLIT], result[:, :SPLIT])
